import numpy as np
import ml_dtypes


def mxq(x, axis, fmt="e4m3"):
    dtype, down = {"e4m3": (ml_dtypes.float8_e4m3fn, 7), "e5m2": (ml_dtypes.float8_e5m2, 14)}[fmt]
    v = np.moveaxis(np.asarray(x, np.float32).astype(ml_dtypes.bfloat16).astype(np.float64), axis, -1)
    blocks = v.reshape(v.shape[:-1] + (-1, 32))
    amax = np.abs(blocks).max(-1, keepdims=True)
    byte = np.maximum(np.where(amax > 0, np.frexp(amax)[1] - 1 + 127, 0) - down, 1)
    scale = np.exp2(byte - 127.0)
    codes = (blocks / scale).astype(np.float32).astype(dtype).astype(np.float64)
    return np.moveaxis((codes * scale).reshape(v.shape), -1, axis)


WIDE = False


def mx_kscale(k):
    if not WIDE:
        return np.ones(k)
    levels = np.array([10, -10, 5, -5, 0])
    if k % 512:
        return np.exp2(np.random.permutation(np.resize(levels, k // 32))).repeat(32)
    a = np.empty((k // 512, 16))
    for p in range(k // 512):
        a[p, :8] = np.random.permutation(np.resize(levels, 8))
        for g in range(8):
            far = levels[np.abs(levels - a[p, g]) >= 10]
            a[p, g + 8] = far[np.random.randint(len(far))]
    return np.exp2(a.ravel()).repeat(32)


def f64(x):
    return np.asarray(x).astype(np.float64)


def striped(idx):
    return np.tile(idx.reshape(-1, 16).T, (8, 1)).astype(np.uint16)


def unstriped(offs):
    return offs[:16].T.reshape(-1).astype(np.int64)


def pack_weight(w):
    k, n = w.shape
    w = f64(np.asarray(w, np.float32).astype(ml_dtypes.bfloat16)).reshape(k // 32, 32, n)
    amax = np.abs(w).max(1)
    byte = np.clip(np.where(amax > 0, np.frexp(amax)[1] - 1 + 127 - 7, 1), 1, 254)
    scaled = (w * np.exp2(127.0 - byte)[:, None, :]).reshape(k, n).astype(np.float32)
    words = np.ascontiguousarray(scaled.reshape(k // 512, 128, 4, n).transpose(0, 1, 3, 2)).astype(ml_dtypes.float8_e4m3fn).view(np.uint8)
    return words, np.ascontiguousarray(byte.astype(np.uint8).reshape(k // 512, 16, n))


def unpack_weight(words, scales):
    g, p, n, _ = words.shape
    vals = np.ascontiguousarray(words).view(ml_dtypes.float8_e4m3fn).astype(np.float64) * np.repeat(np.exp2(scales.astype(np.float64) - 127.0), 8, axis=1)[..., None]
    return vals.transpose(0, 1, 3, 2).reshape(g * 512, n)


K, T, S, N, H, V = 512, 1024, 512, 256, 512, 256


def setup_inputs():
    n = np.random.standard_normal
    s = mx_kscale(K)[:, None]
    u = mx_kscale(H)
    packed_xT = pack_weight(n((K, T)) * s)
    return {
        "x_words": packed_xT[0],
        "x_scales": packed_xT[1],
        "w1": (n((K, H)) / np.sqrt(K) / s).astype(np.float32),
        "t1": (1.2 * n((H, S))).astype(np.float32),
        "unit": (np.random.uniform(0.6, 1.4, (H, 1)) * u[:, None]).astype(np.float32),
        "w2": (n((H, N)) / np.sqrt(H) / u[:, None]).astype(np.float32),
        "offs": striped(np.random.permutation(T)[:S]),
        "qtr": striped(np.random.permutation(S)[:V]),
        "lag": striped(np.random.permutation(S)[:V]),
    }


def reference(x_words, x_scales, w1, t1, unit, w2, offs, qtr, lag):
    xq = unpack_weight(x_words, x_scales)[:, unstriped(offs)]
    y = mxq(f64(w1), 0, "e4m3").T @ xq
    we1 = np.exp(0.8 * (np.tanh(f64(t1))))
    we2 = np.exp(-0.8 * (np.tanh(1.7 * f64(t1))))
    den = we1 + we2 + 1.0
    mid = (y + we1 * (np.pad(y, ((0, 0), (0, 1)))[:, 1:]) + we2 * (np.pad(y, ((0, 0), (0, 2)))[:, 2:])) / den
    zq = mid[:, unstriped(qtr)]
    zl = mid[:, unstriped(lag)]
    gr = zq - (0.7 * zl)
    hid = f64(unit) * gr
    return mxq(f64(w2), 0, "e4m3").T @ mxq(hid, 0, "e4m3")

@@ -1,0 +1,179 @@
+from contextlib import ExitStack
+
+import concourse.mybir as mybir
+from concourse.masks import make_identity
+
+K, T, S, N, H, V = 512, 1024, 512, 256, 512, 256
+FLOPS = 2 * K * H * S + 2 * H * N * V
+
+F32 = mybir.dt.float32
+BF16 = mybir.dt.bfloat16
+I32 = mybir.dt.int32
+U32 = mybir.dt.uint32
+U16 = mybir.dt.uint16
+U8 = mybir.dt.uint8
+FP8X4 = mybir.dt.float8_e4m3fn_x4
+ACT = mybir.ActivationFunctionType
+ALU = mybir.AluOpType
+
+P = 128
+PACK = 4
+EDGE = 8
+
+
+def tile_picked_yalmon_lin_p_kernel(tc, x_words, x_scales, w1, t1, unit, w2, offs, qtr, lag, out):
+    nc = tc.nc
+    with ExitStack() as ctx:
+        keep = ctx.enter_context(tc.tile_pool(name="keep", bufs=1))
+        psum = ctx.enter_context(tc.psum_pool(name="psum", bufs=1))
+
+        offs_sb = keep.tile([P, S // 16], U16, name="offs_sb")
+        qtr_sb = keep.tile([P, V // 16], U16, name="qtr_sb")
+        lag_sb = keep.tile([P, V // 16], U16, name="lag_sb")
+        xw = keep.tile([P, T], I32, name="xw", align_bytes=64)
+        xs = keep.tile([P, T], U8, name="xs", align_bytes=64)
+        t1_sb = [keep.tile([P, S], F32, name="t1_%d" % t) for t in range(PACK)]
+        w1_raw = [keep.tile([P, PACK, H // 2], F32, name="w1_raw%d" % h) for h in range(2)]
+        w2_raw = keep.tile([P, PACK, N], F32, name="w2_raw")
+        unit_sb = keep.tile([P, PACK], F32, name="unit_sb")
+
+        nc.gpsimd.memset(xs[:].bitcast(I32), 0)
+        t1_rows = t1.rearrange("(p t) c -> p t c", t=PACK)
+        w1_rows = w1.rearrange("(p j) c -> p j c", j=PACK)
+        nc.sync.dma_start(out=t1_sb[0][:], in_=t1_rows[:, 0, :])
+        nc.sync.dma_start(out=offs_sb[:], in_=offs)
+        nc.sync.dma_start(out=w1_raw[0][:], in_=w1_rows[:, :, 0 : H // 2])
+        nc.sync.dma_start(out=xw[:], in_=x_words[0].rearrange("p n t -> p (n t)").bitcast(I32))
+        for q in range(4):
+            nc.sync.dma_start(out=xs[32 * q : 32 * q + 4, :].bitcast(I32), in_=x_scales[0][4 * q : 4 * q + 4, :].bitcast(I32))
+        nc.sync.dma_start(out=t1_sb[1][:], in_=t1_rows[:, 1, :])
+        nc.sync.dma_start(out=w1_raw[1][:], in_=w1_rows[:, :, H // 2 : H])
+        nc.sync.dma_start(out=w2_raw[:], in_=w2.rearrange("(p j) c -> p j c", j=PACK))
+        for t in range(2, PACK):
+            nc.sync.dma_start(out=t1_sb[t][:], in_=t1_rows[:, t, :])
+        nc.sync.dma_start(out=unit_sb[:], in_=unit.rearrange("(p t) o -> p (t o)", t=PACK))
+        nc.sync.dma_start(out=lag_sb[:], in_=lag)
+        nc.sync.dma_start(out=qtr_sb[:], in_=qtr)
+
+        ident = keep.tile([P, P], F32, name="ident")
+        make_identity(nc, ident[:])
+
+        prod = [keep.tile([P, 2, S], F32, name="prod%d" % t) for t in range(PACK)]
+        zeros = keep.tile([P, 2, EDGE], F32, name="zeros")
+        nc.gpsimd.memset(zeros[:], 0.0)
+        for t in range(PACK):
+            nc.scalar.activation(out=prod[t][:, :, S - EDGE : S], in_=zeros[:], func=ACT.Copy)
+
+        xg = keep.tile([P, S], U32, name="xg", align_bytes=64)
+        xsg = keep.tile([P, S], U8, name="xsg", align_bytes=64)
+        w1_bf = keep.tile([P, PACK, P, PACK], BF16, name="w1_bf", align_bytes=64)
+        w1_codes = keep.tile([P, H], U32, name="w1_codes", align_bytes=64)
+        w1_scales = keep.tile([P, H], U8, name="w1_scales", align_bytes=64)
+
+        def cast_w1(h):
+            nc.vector.tensor_copy(
+                out=w1_bf[:].rearrange("p t m j -> p m t j")[:, 64 * h : 64 * (h + 1)],
+                in_=w1_raw[h][:].rearrange("p j (m t) -> p m t j", t=PACK),
+            )
+
+        cast_w1(0)
+        nc.vector.tensor_copy(xg[:], xw[:].bitcast(U32).indirect(offs_sb[:]))
+        nc.vector.tensor_copy(xsg[:], xs[:].indirect(offs_sb[:]))
+        cast_w1(1)
+        y = []
+        for t in range(PACK):
+            cols = slice(t * P, (t + 1) * P)
+            nc.vector.quantize_mx(
+                out=w1_codes[:, cols].bitcast(FP8X4),
+                scales=w1_scales[:, cols],
+                in_=w1_bf[:, t].rearrange("p m j -> p (m j)"),
+            )
+            y_t = psum.tile([P, S], F32, name="y%d" % t)
+            nc.tensor.matmul_mx(
+                out=y_t[:],
+                lhsT=w1_codes[:, cols].bitcast(FP8X4),
+                lhsT_scale=w1_scales[:, cols],
+                rhs=xg[:].bitcast(FP8X4),
+                rhs_scale=xsg[:],
+                start=True,
+                stop=True,
+            )
+            y.append(y_t)
+
+        w2_bf = keep.tile([P, N, PACK], BF16, name="w2_bf", align_bytes=64)
+        w2_codes = keep.tile([P, N], U32, name="w2_codes", align_bytes=64)
+        w2_scales = keep.tile([P, N], U8, name="w2_scales", align_bytes=64)
+        nc.vector.tensor_copy(out=w2_bf[:], in_=w2_raw[:].rearrange("p j c -> p c j"))
+        nc.vector.quantize_mx(out=w2_codes[:].bitcast(FP8X4), scales=w2_scales[:], in_=w2_bf[:].rearrange("p c j -> p (c j)"))
+
+        th = [keep.tile([P, 2, S], F32, name="th%d" % t) for t in range(PACK)]
+        we = [keep.tile([P, 2, S], F32, name="we%d" % t) for t in range(PACK)]
+        sq = [keep.tile([P, S], F32, name="sq%d" % t) for t in range(PACK)]
+        num = [keep.tile([P, S], F32, name="num%d" % t) for t in range(PACK)]
+        sums = []
+
+        def square(t):
+            nc.scalar.activation(out=sq[t][:], in_=sums[t][:], func=ACT.Square, bias=1.0)
+
+        for t in range(PACK):
+            nc.scalar.activation(out=th[t][:, 0, :], in_=t1_sb[t][:], func=ACT.Tanh)
+            nc.scalar.activation(out=th[t][:, 1, :], in_=t1_sb[t][:], func=ACT.Tanh, scale=-1.7)
+            nc.scalar.activation(out=we[t][:], in_=th[t][:], func=ACT.Exp, scale=0.8)
+            sum_t = psum.tile([P, S], F32, name="sum%d" % (t % 2))
+            for b in range(S // P):
+                cols = slice(b * P, (b + 1) * P)
+                for k in range(2):
+                    nc.tensor.matmul(out=sum_t[:, cols], lhsT=we[t][:, k, cols], rhs=ident[:], is_transpose=True, start=(k == 0), stop=(k == 1))
+            sums.append(sum_t)
+            if t > 0:
+                square(t - 1)
+
+        for t in range(PACK):
+            nc.vector.tensor_tensor(out=prod[t][:, 0, 0 : S - 1], in0=y[t][:, 1:S], in1=we[t][:, 0, 0 : S - 1], op=ALU.mult)
+            nc.vector.tensor_tensor(out=prod[t][:, 1, 0 : S - 2], in0=y[t][:, 2:S], in1=we[t][:, 1, 0 : S - 2], op=ALU.mult)
+            nc.vector.tensor_tensor(out=t1_sb[t][:], in0=y[t][:], in1=prod[t][:, 0, :], op=ALU.add)
+            nc.gpsimd.tensor_tensor(out=num[t][:], in0=t1_sb[t][:], in1=prod[t][:, 1, :], op=ALU.add)
+
+        rec = [th[PACK - 1][:, 0, :]] + [sq[t][:] for t in range(PACK - 1)]
+        mid = [keep.tile([P, S], F32, name="mid%d" % t) for t in range(PACK)]
+        zl = [keep.tile([P, V], F32, name="zl%d" % t) for t in range(PACK)]
+        hid = keep.tile([P, PACK, V], F32, name="hid")
+        for t in range(PACK):
+            if t == 1:
+                square(PACK - 1)
+            nc.scalar.activation(out=rec[t], in_=sq[t][:], func=ACT.Abs_reciprocal_sqrt)
+        for t in range(PACK):
+            back = psum.tile([P, S], F32, name="y%d" % t)
+            for b in range(S // P):
+                cols = slice(b * P, (b + 1) * P)
+                nc.tensor.transpose(back[:, cols], rec[t][:, cols], ident[:])
+            nc.vector.scalar_tensor_tensor(out=mid[t][:], in0=num[t][:], scalar=unit_sb[:, t : t + 1], in1=back[:], op0=ALU.mult, op1=ALU.mult)
+            nc.scalar.activation(out=zl[t][:], in_=mid[t][:].indirect(lag_sb[:]), func=ACT.Copy, scale=-0.7)
+        for t in range(PACK):
+            nc.vector.tensor_tensor(out=hid[:, t, :], in0=mid[t][:].indirect(qtr_sb[:]), in1=zl[t][:], op=ALU.add)
+
+        hid_bf = keep.tile([P, V, PACK], BF16, name="hid_bf", align_bytes=64)
+        hid_codes = keep.tile([P, V], U32, name="hid_codes", align_bytes=64)
+        hid_scales = keep.tile([P, V], U8, name="hid_scales", align_bytes=64)
+        nc.vector.tensor_copy(out=hid_bf[:], in_=hid[:].rearrange("p t v -> p v t"))
+        nc.vector.quantize_mx(out=hid_codes[:].bitcast(FP8X4), scales=hid_scales[:], in_=hid_bf[:].rearrange("p v t -> p (v t)"))
+
+        for h in range(2):
+            cols = slice(h * P, (h + 1) * P)
+            acc = psum.tile([P, V], F32, name="sum%d" % h)
+            nc.tensor.matmul_mx(
+                out=acc[:],
+                lhsT=w2_codes[:, cols].bitcast(FP8X4),
+                lhsT_scale=w2_scales[:, cols],
+                rhs=hid_codes[:].bitcast(FP8X4),
+                rhs_scale=hid_scales[:],
+                start=True,
+                stop=True,
+            )
+            res = keep.tile([P, V], F32, name="res%d" % h)
+            if h == 0:
+                nc.scalar.copy(out=res[:], in_=acc[:])
+                nc.scalar.dma_start(out=out[cols, :], in_=res[:])
+            else:
+                nc.vector.tensor_copy(out=res[:], in_=acc[:])
+                nc.sync.dma_start(out=out[cols, :], in_=res[:])

@@ -42,15 +42,15 @@ def tile_picked_yalmon_lin_p_kernel(tc, x_words, x_scales, w1, t1, unit, w2, off
         w1_rows = w1.rearrange("(p j) c -> p j c", j=PACK)
         nc.sync.dma_start(out=t1_sb[0][:], in_=t1_rows[:, 0, :])
         nc.sync.dma_start(out=offs_sb[:], in_=offs)
-        nc.sync.dma_start(out=w1_raw[0][:], in_=w1_rows[:, :, 0 : H // 2])
-        nc.sync.dma_start(out=xw[:], in_=x_words[0].rearrange("p n t -> p (n t)").bitcast(I32))
         for q in range(4):
             nc.sync.dma_start(out=xs[32 * q : 32 * q + 4, :].bitcast(I32), in_=x_scales[0][4 * q : 4 * q + 4, :].bitcast(I32))
+        nc.sync.dma_start(out=xw[:], in_=x_words[0].rearrange("p n t -> p (n t)").bitcast(I32))
         nc.sync.dma_start(out=t1_sb[1][:], in_=t1_rows[:, 1, :])
+        nc.sync.dma_start(out=w1_raw[0][:], in_=w1_rows[:, :, 0 : H // 2])
         nc.sync.dma_start(out=w1_raw[1][:], in_=w1_rows[:, :, H // 2 : H])
-        nc.sync.dma_start(out=w2_raw[:], in_=w2.rearrange("(p j) c -> p j c", j=PACK))
         for t in range(2, PACK):
             nc.sync.dma_start(out=t1_sb[t][:], in_=t1_rows[:, t, :])
+        nc.sync.dma_start(out=w2_raw[:], in_=w2.rearrange("(p j) c -> p j c", j=PACK))
         nc.sync.dma_start(out=unit_sb[:], in_=unit.rearrange("(p t) o -> p (t o)", t=PACK))
         nc.sync.dma_start(out=lag_sb[:], in_=lag)
         nc.sync.dma_start(out=qtr_sb[:], in_=qtr)
@@ -70,18 +70,20 @@ def tile_picked_yalmon_lin_p_kernel(tc, x_words, x_scales, w1, t1, unit, w2, off
         w1_codes = keep.tile([P, H], U32, name="w1_codes", align_bytes=64)
         w1_scales = keep.tile([P, H], U8, name="w1_scales", align_bytes=64)
 
-        def cast_w1(h):
+        def cast_w1(h, slots):
             nc.vector.tensor_copy(
-                out=w1_bf[:].rearrange("p t m j -> p m t j")[:, 64 * h : 64 * (h + 1)],
-                in_=w1_raw[h][:].rearrange("p j (m t) -> p m t j", t=PACK),
+                out=w1_bf[:].rearrange("p t m j -> p m t j")[:, 64 * h : 64 * (h + 1), slots],
+                in_=w1_raw[h][:].rearrange("p j (m t) -> p m t j", t=PACK)[:, :, slots],
             )
 
-        cast_w1(0)
-        nc.vector.tensor_copy(xg[:], xw[:].bitcast(U32).indirect(offs_sb[:]))
         nc.vector.tensor_copy(xsg[:], xs[:].indirect(offs_sb[:]))
-        cast_w1(1)
+        nc.vector.tensor_copy(xg[:], xw[:].bitcast(U32).indirect(offs_sb[:]))
+        cast_w1(0, slice(0, PACK))
+        cast_w1(1, slice(0, 1))
         y = []
         for t in range(PACK):
+            if t == 1:
+                cast_w1(1, slice(1, PACK))
             cols = slice(t * P, (t + 1) * P)
             nc.vector.quantize_mx(
                 out=w1_codes[:, cols].bitcast(FP8X4),
@@ -100,33 +102,37 @@ def tile_picked_yalmon_lin_p_kernel(tc, x_words, x_scales, w1, t1, unit, w2, off
             )
             y.append(y_t)
 
-        w2_bf = keep.tile([P, N, PACK], BF16, name="w2_bf", align_bytes=64)
-        w2_codes = keep.tile([P, N], U32, name="w2_codes", align_bytes=64)
-        w2_scales = keep.tile([P, N], U8, name="w2_scales", align_bytes=64)
-        nc.vector.tensor_copy(out=w2_bf[:], in_=w2_raw[:].rearrange("p j c -> p c j"))
-        nc.vector.quantize_mx(out=w2_codes[:].bitcast(FP8X4), scales=w2_scales[:], in_=w2_bf[:].rearrange("p c j -> p (c j)"))
-
         th = [keep.tile([P, 2, S], F32, name="th%d" % t) for t in range(PACK)]
         we = [keep.tile([P, 2, S], F32, name="we%d" % t) for t in range(PACK)]
-        sq = [keep.tile([P, S], F32, name="sq%d" % t) for t in range(PACK)]
-        num = [keep.tile([P, S], F32, name="num%d" % t) for t in range(PACK)]
+        num = [keep.tile([P, S], F32, name="num%d" % t, align_bytes=64) for t in range(PACK)]
+        sq0 = keep.tile([P, S], F32, name="sq0")
+        sq3 = keep.tile([P, S], F32, name="sq3")
+        sq = [sq0[:], th[3][:, 1, :], sq0[:], sq3[:]]
         sums = []
 
         def square(t):
-            nc.scalar.activation(out=sq[t][:], in_=sums[t][:], func=ACT.Square, bias=1.0)
+            nc.scalar.activation(out=sq[t], in_=sums[t][:], func=ACT.Square, bias=1.0)
 
         for t in range(PACK):
             nc.scalar.activation(out=th[t][:, 0, :], in_=t1_sb[t][:], func=ACT.Tanh)
             nc.scalar.activation(out=th[t][:, 1, :], in_=t1_sb[t][:], func=ACT.Tanh, scale=-1.7)
             nc.scalar.activation(out=we[t][:], in_=th[t][:], func=ACT.Exp, scale=0.8)
-            sum_t = psum.tile([P, S], F32, name="sum%d" % (t % 2))
-            for b in range(S // P):
-                cols = slice(b * P, (b + 1) * P)
-                for k in range(2):
-                    nc.tensor.matmul(out=sum_t[:, cols], lhsT=we[t][:, k, cols], rhs=ident[:], is_transpose=True, start=(k == 0), stop=(k == 1))
+            if t < 3:
+                sum_t = psum.tile([P, S], F32, name="sum%d" % t)
+                for b in range(S // P):
+                    cols = slice(b * P, (b + 1) * P)
+                    for k in range(2):
+                        nc.tensor.matmul(out=sum_t[:, cols], lhsT=we[t][:, k, cols], rhs=ident[:], is_transpose=True, start=(k == 0), stop=(k == 1))
+            else:
+                sum_t = keep.tile([P, S], F32, name="sum3")
+                nc.gpsimd.tensor_tensor(out=sum_t[:], in0=we[t][:, 0, :], in1=we[t][:, 1, :], op=ALU.add)
             sums.append(sum_t)
-            if t > 0:
-                square(t - 1)
+            if t == 1:
+                square(0)
+
+        w2_bf = keep.tile([P, N, PACK], BF16, name="w2_bf", align_bytes=64)
+        w2_scales = keep.tile([P, N], U8, name="w2_scales", align_bytes=64)
+        nc.gpsimd.tensor_scalar(out=w2_bf[:], in0=w2_raw[:].rearrange("p j c -> p c j"), scalar1=1.0, scalar2=0.0, op0=ALU.mult, op1=ALU.add)
 
         for t in range(PACK):
             nc.vector.tensor_tensor(out=prod[t][:, 0, 0 : S - 1], in0=y[t][:, 1:S], in1=we[t][:, 0, 0 : S - 1], op=ALU.mult)
@@ -134,46 +140,79 @@ def tile_picked_yalmon_lin_p_kernel(tc, x_words, x_scales, w1, t1, unit, w2, off
             nc.vector.tensor_tensor(out=t1_sb[t][:], in0=y[t][:], in1=prod[t][:, 0, :], op=ALU.add)
             nc.gpsimd.tensor_tensor(out=num[t][:], in0=t1_sb[t][:], in1=prod[t][:, 1, :], op=ALU.add)
 
-        rec = [th[PACK - 1][:, 0, :]] + [sq[t][:] for t in range(PACK - 1)]
+        rec = [th[3][:, 0, :]] + [th[t][:, 0, :] for t in range(3)]
         mid = [keep.tile([P, S], F32, name="mid%d" % t) for t in range(PACK)]
         zl = [keep.tile([P, V], F32, name="zl%d" % t) for t in range(PACK)]
         hid = keep.tile([P, PACK, V], F32, name="hid")
-        for t in range(PACK):
-            if t == 1:
-                square(PACK - 1)
-            nc.scalar.activation(out=rec[t], in_=sq[t][:], func=ACT.Abs_reciprocal_sqrt)
-        for t in range(PACK):
-            back = psum.tile([P, S], F32, name="y%d" % t)
-            for b in range(S // P):
-                cols = slice(b * P, (b + 1) * P)
-                nc.tensor.transpose(back[:, cols], rec[t][:, cols], ident[:])
-            nc.vector.scalar_tensor_tensor(out=mid[t][:], in0=num[t][:], scalar=unit_sb[:, t : t + 1], in1=back[:], op0=ALU.mult, op1=ALU.mult)
+
+        def invert(t):
+            nc.scalar.activation(out=rec[t], in_=sq[t], func=ACT.Abs_reciprocal_sqrt)
+
+        def normalise(t):
+            if t < 3:
+                back = psum.tile([P, S], F32, name="y%d" % t)
+                for b in range(S // P):
+                    cols = slice(b * P, (b + 1) * P)
+                    nc.tensor.transpose(back[:, cols], rec[t][:, cols], ident[:])
+                r = back[:]
+            else:
+                r = rec[t]
+            nc.vector.scalar_tensor_tensor(out=mid[t][:], in0=num[t][:], scalar=unit_sb[:, t : t + 1], in1=r, op0=ALU.mult, op1=ALU.mult)
+
+        def fetch_lag(t):
             nc.scalar.activation(out=zl[t][:], in_=mid[t][:].indirect(lag_sb[:]), func=ACT.Copy, scale=-0.7)
-        for t in range(PACK):
+
+        def fetch_qtr(t):
             nc.vector.tensor_tensor(out=hid[:, t, :], in0=mid[t][:].indirect(qtr_sb[:]), in1=zl[t][:], op=ALU.add)
 
-        hid_bf = keep.tile([P, V, PACK], BF16, name="hid_bf", align_bytes=64)
-        hid_codes = keep.tile([P, V], U32, name="hid_codes", align_bytes=64)
-        hid_scales = keep.tile([P, V], U8, name="hid_scales", align_bytes=64)
-        nc.vector.tensor_copy(out=hid_bf[:], in_=hid[:].rearrange("p t v -> p v t"))
-        nc.vector.quantize_mx(out=hid_codes[:].bitcast(FP8X4), scales=hid_scales[:], in_=hid_bf[:].rearrange("p v t -> p (v t)"))
+        invert(0)
+        square(1)
+        square(2)
+        normalise(0)
+        w2_codes = keep.tile([P, N], U32, name="num0", align_bytes=64)
+        nc.vector.quantize_mx(out=w2_codes[:].bitcast(FP8X4), scales=w2_scales[:], in_=w2_bf[:].rearrange("p c j -> p (c j)"))
+        invert(1)
+        invert(2)
+        square(3)
+        normalise(1)
+        fetch_lag(0)
+        invert(3)
+        normalise(2)
+        fetch_lag(1)
+        fetch_qtr(0)
+        normalise(3)
+        fetch_lag(2)
+        fetch_qtr(1)
+        fetch_lag(3)
+        fetch_qtr(2)
+        for g in range(2):
+            cols = slice(g * P, (g + 1) * P)
+            nc.vector.tensor_tensor(out=hid[:, 3, cols], in0=mid[3][:].indirect(qtr_sb[:, 8 * g : 8 * (g + 1)]), in1=zl[3][:, cols], op=ALU.add)
 
-        for h in range(2):
-            cols = slice(h * P, (h + 1) * P)
-            acc = psum.tile([P, V], F32, name="sum%d" % h)
-            nc.tensor.matmul_mx(
-                out=acc[:],
-                lhsT=w2_codes[:, cols].bitcast(FP8X4),
-                lhsT_scale=w2_scales[:, cols],
-                rhs=hid_codes[:].bitcast(FP8X4),
-                rhs_scale=hid_scales[:],
-                start=True,
-                stop=True,
-            )
-            res = keep.tile([P, V], F32, name="res%d" % h)
-            if h == 0:
+        out_rows = out.rearrange("(h p) v -> p h v", p=P)
+        hid_bf = [keep.tile([P, P, PACK], BF16, name="hid_bf%d" % g, align_bytes=64) for g in range(2)]
+        hid_codes = [keep.tile([P, P], U32, name="hid_codes%d" % g, align_bytes=64) for g in range(2)]
+        hid_scales = [keep.tile([P, P], U8, name="hid_scales%d" % g, align_bytes=64) for g in range(2)]
+        nc.scalar.copy(out=hid_bf[0][:], in_=hid[:, :, 0:P].rearrange("p t v -> p v t"))
+        nc.vector.tensor_copy(out=hid_bf[1][:], in_=hid[:, :, P : 2 * P].rearrange("p t v -> p v t"))
+        for g in range(2):
+            nc.vector.quantize_mx(out=hid_codes[g][:].bitcast(FP8X4), scales=hid_scales[g][:], in_=hid_bf[g][:].rearrange("p v t -> p (v t)"))
+            acc = psum.tile([P, 2, P], F32, name="sum%d" % g)
+            for h in range(2):
+                cols = slice(h * P, (h + 1) * P)
+                nc.tensor.matmul_mx(
+                    out=acc[:, h, :],
+                    lhsT=w2_codes[:, cols].bitcast(FP8X4),
+                    lhsT_scale=w2_scales[:, cols],
+                    rhs=hid_codes[g][:].bitcast(FP8X4),
+                    rhs_scale=hid_scales[g][:],
+                    start=True,
+                    stop=True,
+                )
+            res = keep.tile([P, 2, P], F32, name="res%d" % g)
+            if g == 0:
                 nc.scalar.copy(out=res[:], in_=acc[:])
-                nc.scalar.dma_start(out=out[cols, :], in_=res[:])
+                nc.scalar.dma_start(out=out_rows[:, :, g * P : (g + 1) * P], in_=res[:])
             else:
                 nc.vector.tensor_copy(out=res[:], in_=acc[:])
-                nc.sync.dma_start(out=out[cols, :], in_=res[:])
+                nc.sync.dma_start(out=out_rows[:, :, g * P : (g + 1) * P], in_=res[:])

@@ -41,10 +41,10 @@ def tile_picked_yalmon_lin_p_kernel(tc, x_words, x_scales, w1, t1, unit, w2, off
         t1_rows = t1.rearrange("(p t) c -> p t c", t=PACK)
         w1_rows = w1.rearrange("(p j) c -> p j c", j=PACK)
         nc.sync.dma_start(out=t1_sb[0][:], in_=t1_rows[:, 0, :])
+        nc.sync.dma_start(out=xw[:], in_=x_words[0].rearrange("p n t -> p (n t)").bitcast(I32))
         nc.sync.dma_start(out=offs_sb[:], in_=offs)
         for q in range(4):
             nc.sync.dma_start(out=xs[32 * q : 32 * q + 4, :].bitcast(I32), in_=x_scales[0][4 * q : 4 * q + 4, :].bitcast(I32))
-        nc.sync.dma_start(out=xw[:], in_=x_words[0].rearrange("p n t -> p (n t)").bitcast(I32))
         nc.sync.dma_start(out=t1_sb[1][:], in_=t1_rows[:, 1, :])
         nc.sync.dma_start(out=w1_raw[0][:], in_=w1_rows[:, :, 0 : H // 2])
         nc.sync.dma_start(out=w1_raw[1][:], in_=w1_rows[:, :, H // 2 : H])
@@ -76,8 +76,8 @@ def tile_picked_yalmon_lin_p_kernel(tc, x_words, x_scales, w1, t1, unit, w2, off
                 in_=w1_raw[h][:].rearrange("p j (m t) -> p m t j", t=PACK)[:, :, slots],
             )
 
-        nc.vector.tensor_copy(xsg[:], xs[:].indirect(offs_sb[:]))
         nc.vector.tensor_copy(xg[:], xw[:].bitcast(U32).indirect(offs_sb[:]))
+        nc.vector.tensor_copy(xsg[:], xs[:].indirect(offs_sb[:]))
         cast_w1(0, slice(0, PACK))
         cast_w1(1, slice(0, 1))
         y = []

from contextlib import ExitStack

import concourse.mybir as mybir
from concourse.masks import make_identity

K, T, S, N, H, V = 512, 1024, 512, 256, 512, 256
FLOPS = 2 * K * H * S + 2 * H * N * V

F32 = mybir.dt.float32
BF16 = mybir.dt.bfloat16
I32 = mybir.dt.int32
U32 = mybir.dt.uint32
U16 = mybir.dt.uint16
U8 = mybir.dt.uint8
FP8X4 = mybir.dt.float8_e4m3fn_x4
ACT = mybir.ActivationFunctionType
ALU = mybir.AluOpType

P = 128
PACK = 4
EDGE = 8


def tile_picked_yalmon_lin_p_kernel(tc, x_words, x_scales, w1, t1, unit, w2, offs, qtr, lag, out):
    nc = tc.nc
    with ExitStack() as ctx:
        keep = ctx.enter_context(tc.tile_pool(name="keep", bufs=1))
        psum = ctx.enter_context(tc.psum_pool(name="psum", bufs=1))

        offs_sb = keep.tile([P, S // 16], U16, name="offs_sb")
        qtr_sb = keep.tile([P, V // 16], U16, name="qtr_sb")
        lag_sb = keep.tile([P, V // 16], U16, name="lag_sb")
        xw = keep.tile([P, T], I32, name="xw", align_bytes=64)
        xs = keep.tile([P, T], U8, name="xs", align_bytes=64)
        t1_sb = [keep.tile([P, S], F32, name="t1_%d" % t) for t in range(PACK)]
        w1_raw = [keep.tile([P, PACK, H // 2], F32, name="w1_raw%d" % h) for h in range(2)]
        w2_raw = keep.tile([P, PACK, N], F32, name="w2_raw")
        unit_sb = keep.tile([P, PACK], F32, name="unit_sb")

        nc.gpsimd.memset(xs[:].bitcast(I32), 0)
        t1_rows = t1.rearrange("(p t) c -> p t c", t=PACK)
        w1_rows = w1.rearrange("(p j) c -> p j c", j=PACK)
        nc.sync.dma_start(out=t1_sb[0][:], in_=t1_rows[:, 0, :])
        nc.sync.dma_start(out=xw[:], in_=x_words[0].rearrange("p n t -> p (n t)").bitcast(I32))
        nc.sync.dma_start(out=offs_sb[:], in_=offs)
        for q in range(4):
            nc.sync.dma_start(out=xs[32 * q : 32 * q + 4, :].bitcast(I32), in_=x_scales[0][4 * q : 4 * q + 4, :].bitcast(I32))
        nc.sync.dma_start(out=t1_sb[1][:], in_=t1_rows[:, 1, :])
        nc.sync.dma_start(out=w1_raw[0][:], in_=w1_rows[:, :, 0 : H // 2])
        nc.sync.dma_start(out=w1_raw[1][:], in_=w1_rows[:, :, H // 2 : H])
        for t in range(2, PACK):
            nc.sync.dma_start(out=t1_sb[t][:], in_=t1_rows[:, t, :])
        nc.sync.dma_start(out=w2_raw[:], in_=w2.rearrange("(p j) c -> p j c", j=PACK))
        nc.sync.dma_start(out=unit_sb[:], in_=unit.rearrange("(p t) o -> p (t o)", t=PACK))
        nc.sync.dma_start(out=lag_sb[:], in_=lag)
        nc.sync.dma_start(out=qtr_sb[:], in_=qtr)

        ident = keep.tile([P, P], F32, name="ident")
        make_identity(nc, ident[:])

        prod = [keep.tile([P, 2, S], F32, name="prod%d" % t) for t in range(PACK)]
        zeros = keep.tile([P, 2, EDGE], F32, name="zeros")
        nc.gpsimd.memset(zeros[:], 0.0)
        for t in range(PACK):
            nc.scalar.activation(out=prod[t][:, :, S - EDGE : S], in_=zeros[:], func=ACT.Copy)

        xg = keep.tile([P, S], U32, name="xg", align_bytes=64)
        xsg = keep.tile([P, S], U8, name="xsg", align_bytes=64)
        w1_bf = keep.tile([P, PACK, P, PACK], BF16, name="w1_bf", align_bytes=64)
        w1_codes = keep.tile([P, H], U32, name="w1_codes", align_bytes=64)
        w1_scales = keep.tile([P, H], U8, name="w1_scales", align_bytes=64)

        def cast_w1(h, slots):
            nc.vector.tensor_copy(
                out=w1_bf[:].rearrange("p t m j -> p m t j")[:, 64 * h : 64 * (h + 1), slots],
                in_=w1_raw[h][:].rearrange("p j (m t) -> p m t j", t=PACK)[:, :, slots],
            )

        nc.vector.tensor_copy(xg[:], xw[:].bitcast(U32).indirect(offs_sb[:]))
        nc.vector.tensor_copy(xsg[:], xs[:].indirect(offs_sb[:]))
        cast_w1(0, slice(0, PACK))
        cast_w1(1, slice(0, 1))
        y = []
        for t in range(PACK):
            if t == 1:
                cast_w1(1, slice(1, PACK))
            cols = slice(t * P, (t + 1) * P)
            nc.vector.quantize_mx(
                out=w1_codes[:, cols].bitcast(FP8X4),
                scales=w1_scales[:, cols],
                in_=w1_bf[:, t].rearrange("p m j -> p (m j)"),
            )
            y_t = psum.tile([P, S], F32, name="y%d" % t)
            nc.tensor.matmul_mx(
                out=y_t[:],
                lhsT=w1_codes[:, cols].bitcast(FP8X4),
                lhsT_scale=w1_scales[:, cols],
                rhs=xg[:].bitcast(FP8X4),
                rhs_scale=xsg[:],
                start=True,
                stop=True,
            )
            y.append(y_t)

        th = [keep.tile([P, 2, S], F32, name="th%d" % t) for t in range(PACK)]
        we = [keep.tile([P, 2, S], F32, name="we%d" % t) for t in range(PACK)]
        num = [keep.tile([P, S], F32, name="num%d" % t, align_bytes=64) for t in range(PACK)]
        sq0 = keep.tile([P, S], F32, name="sq0")
        sq3 = keep.tile([P, S], F32, name="sq3")
        sq = [sq0[:], th[3][:, 1, :], sq0[:], sq3[:]]
        sums = []

        def square(t):
            nc.scalar.activation(out=sq[t], in_=sums[t][:], func=ACT.Square, bias=1.0)

        for t in range(PACK):
            nc.scalar.activation(out=th[t][:, 0, :], in_=t1_sb[t][:], func=ACT.Tanh)
            nc.scalar.activation(out=th[t][:, 1, :], in_=t1_sb[t][:], func=ACT.Tanh, scale=-1.7)
            nc.scalar.activation(out=we[t][:], in_=th[t][:], func=ACT.Exp, scale=0.8)
            if t < 3:
                sum_t = psum.tile([P, S], F32, name="sum%d" % t)
                for b in range(S // P):
                    cols = slice(b * P, (b + 1) * P)
                    for k in range(2):
                        nc.tensor.matmul(out=sum_t[:, cols], lhsT=we[t][:, k, cols], rhs=ident[:], is_transpose=True, start=(k == 0), stop=(k == 1))
            else:
                sum_t = keep.tile([P, S], F32, name="sum3")
                nc.gpsimd.tensor_tensor(out=sum_t[:], in0=we[t][:, 0, :], in1=we[t][:, 1, :], op=ALU.add)
            sums.append(sum_t)
            if t == 1:
                square(0)

        w2_bf = keep.tile([P, N, PACK], BF16, name="w2_bf", align_bytes=64)
        w2_scales = keep.tile([P, N], U8, name="w2_scales", align_bytes=64)
        nc.gpsimd.tensor_scalar(out=w2_bf[:], in0=w2_raw[:].rearrange("p j c -> p c j"), scalar1=1.0, scalar2=0.0, op0=ALU.mult, op1=ALU.add)

        for t in range(PACK):
            nc.vector.tensor_tensor(out=prod[t][:, 0, 0 : S - 1], in0=y[t][:, 1:S], in1=we[t][:, 0, 0 : S - 1], op=ALU.mult)
            nc.vector.tensor_tensor(out=prod[t][:, 1, 0 : S - 2], in0=y[t][:, 2:S], in1=we[t][:, 1, 0 : S - 2], op=ALU.mult)
            nc.vector.tensor_tensor(out=t1_sb[t][:], in0=y[t][:], in1=prod[t][:, 0, :], op=ALU.add)
            nc.gpsimd.tensor_tensor(out=num[t][:], in0=t1_sb[t][:], in1=prod[t][:, 1, :], op=ALU.add)

        rec = [th[3][:, 0, :]] + [th[t][:, 0, :] for t in range(3)]
        mid = [keep.tile([P, S], F32, name="mid%d" % t) for t in range(PACK)]
        zl = [keep.tile([P, V], F32, name="zl%d" % t) for t in range(PACK)]
        hid = keep.tile([P, PACK, V], F32, name="hid")

        def invert(t):
            nc.scalar.activation(out=rec[t], in_=sq[t], func=ACT.Abs_reciprocal_sqrt)

        def normalise(t):
            if t < 3:
                back = psum.tile([P, S], F32, name="y%d" % t)
                for b in range(S // P):
                    cols = slice(b * P, (b + 1) * P)
                    nc.tensor.transpose(back[:, cols], rec[t][:, cols], ident[:])
                r = back[:]
            else:
                r = rec[t]
            nc.vector.scalar_tensor_tensor(out=mid[t][:], in0=num[t][:], scalar=unit_sb[:, t : t + 1], in1=r, op0=ALU.mult, op1=ALU.mult)

        def fetch_lag(t):
            nc.scalar.activation(out=zl[t][:], in_=mid[t][:].indirect(lag_sb[:]), func=ACT.Copy, scale=-0.7)

        def fetch_qtr(t):
            nc.vector.tensor_tensor(out=hid[:, t, :], in0=mid[t][:].indirect(qtr_sb[:]), in1=zl[t][:], op=ALU.add)

        invert(0)
        square(1)
        square(2)
        normalise(0)
        w2_codes = keep.tile([P, N], U32, name="num0", align_bytes=64)
        nc.vector.quantize_mx(out=w2_codes[:].bitcast(FP8X4), scales=w2_scales[:], in_=w2_bf[:].rearrange("p c j -> p (c j)"))
        invert(1)
        invert(2)
        square(3)
        normalise(1)
        fetch_lag(0)
        invert(3)
        normalise(2)
        fetch_lag(1)
        fetch_qtr(0)
        normalise(3)
        fetch_lag(2)
        fetch_qtr(1)
        fetch_lag(3)
        fetch_qtr(2)
        for g in range(2):
            cols = slice(g * P, (g + 1) * P)
            nc.vector.tensor_tensor(out=hid[:, 3, cols], in0=mid[3][:].indirect(qtr_sb[:, 8 * g : 8 * (g + 1)]), in1=zl[3][:, cols], op=ALU.add)

        out_rows = out.rearrange("(h p) v -> p h v", p=P)
        hid_bf = [keep.tile([P, P, PACK], BF16, name="hid_bf%d" % g, align_bytes=64) for g in range(2)]
        hid_codes = [keep.tile([P, P], U32, name="hid_codes%d" % g, align_bytes=64) for g in range(2)]
        hid_scales = [keep.tile([P, P], U8, name="hid_scales%d" % g, align_bytes=64) for g in range(2)]
        nc.scalar.copy(out=hid_bf[0][:], in_=hid[:, :, 0:P].rearrange("p t v -> p v t"))
        nc.vector.tensor_copy(out=hid_bf[1][:], in_=hid[:, :, P : 2 * P].rearrange("p t v -> p v t"))
        for g in range(2):
            nc.vector.quantize_mx(out=hid_codes[g][:].bitcast(FP8X4), scales=hid_scales[g][:], in_=hid_bf[g][:].rearrange("p v t -> p (v t)"))
            acc = psum.tile([P, 2, P], F32, name="sum%d" % g)
            for h in range(2):
                cols = slice(h * P, (h + 1) * P)
                nc.tensor.matmul_mx(
                    out=acc[:, h, :],
                    lhsT=w2_codes[:, cols].bitcast(FP8X4),
                    lhsT_scale=w2_scales[:, cols],
                    rhs=hid_codes[g][:].bitcast(FP8X4),
                    rhs_scale=hid_scales[g][:],
                    start=True,
                    stop=True,
                )
            res = keep.tile([P, 2, P], F32, name="res%d" % g)
            if g == 0:
                nc.scalar.copy(out=res[:], in_=acc[:])
                nc.scalar.dma_start(out=out_rows[:, :, g * P : (g + 1) * P], in_=res[:])
            else:
                nc.vector.tensor_copy(out=res[:], in_=acc[:])
                nc.sync.dma_start(out=out_rows[:, :, g * P : (g + 1) * P], in_=res[:])
